import numpy as np
import ml_dtypes


def mxq(x, axis, fmt="e4m3"):
    dtype, down = {"e4m3": (ml_dtypes.float8_e4m3fn, 7), "e5m2": (ml_dtypes.float8_e5m2, 14)}[fmt]
    v = np.moveaxis(np.asarray(x, np.float32).astype(ml_dtypes.bfloat16).astype(np.float64), axis, -1)
    blocks = v.reshape(v.shape[:-1] + (-1, 32))
    amax = np.abs(blocks).max(-1, keepdims=True)
    byte = np.maximum(np.where(amax > 0, np.frexp(amax)[1] - 1 + 127, 0) - down, 1)
    scale = np.exp2(byte - 127.0)
    codes = (blocks / scale).astype(np.float32).astype(dtype).astype(np.float64)
    return np.moveaxis((codes * scale).reshape(v.shape), -1, axis)


WIDE = False


def mx_kscale(k, group=512):
    if not WIDE:
        return np.ones(k)
    levels = np.array([18, -18])
    if group != 512:
        return np.exp2(np.random.permutation(np.resize(levels, k // group))).repeat(group)
    if k % 512:
        return np.exp2(np.random.permutation(np.resize(levels, k // 32))).repeat(32)
    a = np.empty((k // 512, 16))
    for p in range(k // 512):
        a[p, :8] = np.random.permutation(np.resize(levels, 8))
        for g in range(8):
            far = levels[np.abs(levels - a[p, g]) >= 10]
            a[p, g + 8] = far[np.random.randint(len(far))]
    return np.exp2(a.ravel()).repeat(32)


def f64(x):
    return np.asarray(x).astype(np.float64)


E2M1 = np.array([0.0, 0.5, 1.0, 1.5, 2.0, 3.0, 4.0, 6.0, -0.0, -0.5, -1.0, -1.5, -2.0, -3.0, -4.0, -6.0])


def pack_group(w):
    k, n = w.shape
    w = f64(np.asarray(w, np.float32).astype(ml_dtypes.bfloat16)).reshape(k // 32, 32, n)
    amax = np.abs(w).max(1)
    mant, ex = np.frexp(amax / 6.0)
    byte = np.clip(np.where(amax > 0, np.where(mant > 0.5, ex, ex - 1) + 127, 1), 1, 254)
    scaled = (w * np.exp2(127.0 - byte)[:, None, :]).reshape(k, n).astype(np.float32)
    c = np.ascontiguousarray(scaled.reshape(k // 4, 4, n).transpose(0, 2, 1)).astype(ml_dtypes.float4_e2m1fn).view(np.uint8) & 0xF
    return np.ascontiguousarray((c[..., 0::2] | (c[..., 1::2] << 4)).reshape(k // 4, 2 * n)), byte.astype(np.uint8)


def unpack_group(words, scales):
    p, n = words.shape[0], scales.shape[1]
    words = np.ascontiguousarray(words).reshape(p, n, 2)
    nib = np.empty((p, n, 4), np.uint8)
    nib[..., 0::2] = words & 0xF
    nib[..., 1::2] = words >> 4
    return E2M1[nib].transpose(0, 2, 1).reshape(4 * p, n) * np.repeat(np.exp2(scales.astype(np.float64) - 127.0), 32, axis=0)


def silu(v):
    return v / (1.0 + np.exp(-v))


G, D, M, N = 4, 128, 256, 1024


def setup_inputs():
    n = np.random.standard_normal
    s = mx_kscale(D, 0)[:, None]
    w_ = [pack_group(w) for w in n((G, D, M)) / np.sqrt(D) / s]
    return {
        "x": (n((G, D, N)) * s).astype(np.float32),
        "w_words": np.stack([w[0] for w in w_]),
        "w_scales": np.stack([w[1] for w in w_]),
    }


def reference(x, w_words, w_scales):
    xq = mxq(f64(x), 1, "e4m3")
    y = np.stack([unpack_group(w_words[g], w_scales[g]) for g in range(G)]).transpose(0, 2, 1) @ xq
    y = silu(y)
    return y

@@ -1,0 +1,183 @@
+from contextlib import ExitStack
+
+import concourse.mybir as mybir
+
+G, D, M, N = 4, 128, 256, 1024
+FLOPS = 2 * G * D * M * N
+
+F32 = mybir.dt.float32
+BF16 = mybir.dt.bfloat16
+I32 = mybir.dt.int32
+U32 = mybir.dt.uint32
+U8 = mybir.dt.uint8
+FP8X4 = mybir.dt.float8_e4m3fn_x4
+FP4X4 = mybir.dt.float4_e2m1fn_x4
+ACT = mybir.ActivationFunctionType
+
+P = 128
+ROWS = 32
+PACK = 4
+WINDOW = 512
+PAD = 256
+LOADS = [[0,256],[256,512],[512,1024]]
+PROGRAM = [["load",0,"sp"],
+    ["warm"],
+    ["words","sp"],
+    ["wscale",0,"sp"],
+    ["wscale",1,"sp"],
+    ["wscale",2,"sp"],
+    ["wscale",3,"sp"],
+    ["load",1,"sp"],
+    ["load",2,"sp"],
+    ["cast",0,168,"v"],
+    ["cast",168,256,"a"],
+    ["quant",0,256],
+    ["mm",0,0,0,256],
+    ["silu",0,0,0,0,256,256],
+    ["store",0,0,0,256,"sp"],
+    ["mm",1,0,0,256],
+    ["silu",1,0,0,0,256,256],
+    ["store",1,0,0,256,"sp"],
+    ["mm",2,0,0,256],
+    ["silu",2,0,0,0,256,256],
+    ["store",2,0,0,256,"sp"],
+    ["mm",3,0,0,256],
+    ["silu",3,0,0,0,256,256],
+    ["mm",0,1,1,256],
+    ["silu",0,1,1,0,256,256],
+    ["mm",1,1,1,256],
+    ["silu",1,1,1,0,256,256],
+    ["cast",256,512,"v"],
+    ["quant",256,512],
+    ["mm",2,1,1,512],
+    ["silu",2,1,1,0,512,512],
+    ["store",2,1,0,512,"sp"],
+    ["mm",3,0,1,512],
+    ["silu",3,0,1,256,512,512],
+    ["store",3,0,0,512,"sp"],
+    ["mm",0,1,0,512],
+    ["silu",0,1,0,256,512,512],
+    ["store",0,1,0,512,"sp"],
+    ["mm",1,1,0,512],
+    ["silu",1,1,0,256,512,512],
+    ["store",1,1,0,512,"sp"],
+    ["mm",3,1,0,512],
+    ["silu",3,1,0,0,512,512],
+    ["store",3,1,0,512,"sp"],
+    ["cast",512,768,"v"],
+    ["quant",512,768],
+    ["cast",768,1024,"v"],
+    ["quant",768,1024],
+    ["mm",0,0,1,768],
+    ["silu",0,0,1,256,768,768],
+    ["mm",1,0,1,768],
+    ["silu",1,0,1,256,768,768],
+    ["mm",2,0,0,768],
+    ["silu",2,0,0,256,768,768],
+    ["mm",0,0,0,1024],
+    ["silu",0,0,0,768,1024,1024],
+    ["store",0,0,256,1024,"sp"],
+    ["mm",1,0,0,1024],
+    ["silu",1,0,0,768,1024,1024],
+    ["store",1,0,256,1024,"sp"],
+    ["mm",2,0,1,1024],
+    ["silu",2,0,1,768,1024,1024],
+    ["store",2,0,256,1024,"sp"],
+    ["mm",3,0,1,1024],
+    ["silu",3,0,1,512,1024,1024],
+    ["store",3,0,512,1024,"sp"],
+    ["mm",0,1,1,1024],
+    ["silu",0,1,1,512,1024,1024],
+    ["store",0,1,512,1024,"sp"],
+    ["mm",1,1,1,1024],
+    ["silu",1,1,1,512,1024,1024],
+    ["store",1,1,512,1024,"sp"],
+    ["mm",2,1,0,1024],
+    ["silu",2,1,0,512,1024,1024],
+    ["store",2,1,512,1024,"sp"],
+    ["mm",3,1,0,1024],
+    ["silu",3,1,0,512,1024,1024],
+    ["store",3,1,512,1024,"sp"]]
+
+
+def tile_rows_glin_silu_kernel(tc, x, w_words, w_scales, out):
+    nc = tc.nc
+    with ExitStack() as ctx:
+        keep = ctx.enter_context(tc.tile_pool(name="keep", bufs=1))
+        psum = ctx.enter_context(tc.psum_pool(name="psum", bufs=1))
+        ctx.enter_context(tc.manual_schedule())
+
+        x_rows = x.rearrange("g (p j) n -> (g p) j n", j=PACK)
+        raw = [keep.tile([P, PACK, c1 - c0], F32, name="raw%d" % c0, align_bytes=64) for c0, c1 in LOADS]
+        grouped = keep.tile([P, N, PACK], BF16, align_bytes=64)
+        codes = keep.tile([P, PAD + N], U32, align_bytes=64)
+        scales = keep.tile([P, PAD + N], U8, align_bytes=64)
+        words = keep.tile([P, 2 * M], U8, align_bytes=64)
+        wscales = keep.tile([P, M], U8, align_bytes=64)
+        warm_in = keep.tile([P, 8], F32)
+        warm_out = keep.tile([P, 8], F32)
+        result = {(g, t): keep.tile([P, N], F32, name="res%d%d" % (g, t), align_bytes=64) for g in range(G) for t in range(2)}
+        banks = {(g, b): psum.tile([P, WINDOW], F32, name="bank%d%d" % (g, b)) for g in range(G) for b in range(2)}
+        queues = {"sp": nc.sync, "act": nc.scalar, "pool": nc.gpsimd}
+
+        nc.vector.memset(warm_in[:], 0.0)
+        nc.vector.memset(wscales[:].bitcast(I32), 0)
+        nc.vector.memset(scales[:, 0:PAD].bitcast(I32), 0)
+        nc.vector.memset(codes[:, 0:PAD], 0)
+
+        def source(c0, c1):
+            for (l0, l1), t in zip(LOADS, raw):
+                if l0 <= c0 and c1 <= l1:
+                    return t[:, :, c0 - l0 : c1 - l0]
+            raise ValueError("no such load")
+
+        for step in PROGRAM:
+            kind = step[0]
+            if kind == "warm":
+                nc.scalar.activation(out=warm_out[:, 0:1], in_=warm_in[:, 0:1], func=ACT.Silu)
+            elif kind == "load":
+                c0, c1 = LOADS[step[1]]
+                queues[step[2]].dma_start(out=raw[step[1]][:], in_=x_rows[:, :, c0:c1])
+            elif kind == "words":
+                queues[step[1]].dma_start(out=words[:].bitcast(I32), in_=w_words.rearrange("g p b -> (g p) b").bitcast(I32))
+            elif kind == "wscale":
+                g = step[1]
+                queues[step[2]].dma_start(out=wscales[ROWS * g : ROWS * g + 4, :].bitcast(I32), in_=w_scales[g].bitcast(I32))
+            elif kind == "cast":
+                c0, c1 = step[1], step[2]
+                dst = grouped[:, c0:c1, :].rearrange("p (c i) t -> p c t i", i=4)
+                src = source(c0, c1).rearrange("p t (c i) -> p c t i", i=4)
+                if step[3] == "v":
+                    nc.vector.tensor_copy(out=dst, in_=src)
+                else:
+                    nc.scalar.copy(out=dst, in_=src)
+            elif kind == "quant":
+                c0, c1 = step[1], step[2]
+                nc.vector.quantize_mx(
+                    out=codes[:, PAD + c0 : PAD + c1].bitcast(FP8X4),
+                    scales=scales[:, PAD + c0 : PAD + c1],
+                    in_=grouped[:, c0:c1, :].rearrange("p c t -> p (c t)"),
+                )
+            elif kind == "mm":
+                g, t, b, c1 = step[1:]
+                rows = slice(ROWS * g, ROWS * (g + 1))
+                cols = slice(PAD + c1 - WINDOW, PAD + c1)
+                nc.tensor.matmul_mx(
+                    out=banks[g, b][:],
+                    lhsT=words[rows, 2 * P * t : 2 * P * (t + 1)].bitcast(FP4X4),
+                    lhsT_scale=wscales[rows, P * t : P * (t + 1)],
+                    rhs=codes[rows, cols].bitcast(FP8X4),
+                    rhs_scale=scales[rows, cols],
+                    start=True,
+                    stop=True,
+                )
+            elif kind == "silu":
+                g, t, b, c0, c1, end = step[1:]
+                nc.scalar.activation(
+                    out=result[g, t][:, c0:c1],
+                    in_=banks[g, b][:, WINDOW - (end - c0) : WINDOW - (end - c1)],
+                    func=ACT.Silu,
+                )
+            else:
+                g, t, c0, c1 = step[1:5]
+                queues[step[5]].dma_start(out=out[g, P * t : P * (t + 1), c0:c1], in_=result[g, t][:, c0:c1])

@@ -32,59 +32,48 @@ PROGRAM = [["load",0,"sp"],
     ["cast",0,168,"v"],
     ["cast",168,256,"a"],
     ["quant",0,256],
+    ["cast",256,424,"v"],
+    ["cast",424,512,"a"],
     ["mm",0,0,0,256],
     ["silu",0,0,0,0,256,256],
     ["store",0,0,0,256,"sp"],
     ["mm",1,0,0,256],
     ["silu",1,0,0,0,256,256],
     ["store",1,0,0,256,"sp"],
-    ["mm",2,0,0,256],
-    ["silu",2,0,0,0,256,256],
-    ["store",2,0,0,256,"sp"],
-    ["mm",3,0,0,256],
-    ["silu",3,0,0,0,256,256],
-    ["mm",0,1,1,256],
-    ["silu",0,1,1,0,256,256],
-    ["mm",1,1,1,256],
-    ["silu",1,1,1,0,256,256],
-    ["cast",256,512,"v"],
     ["quant",256,512],
+    ["mm",2,0,0,512],
+    ["silu",2,0,0,0,512,512],
+    ["store",2,0,0,512,"sp"],
+    ["mm",3,0,0,512],
+    ["silu",3,0,0,0,512,512],
+    ["store",3,0,0,512,"sp"],
+    ["mm",0,1,1,512],
+    ["silu",0,1,1,0,512,512],
+    ["store",0,1,0,512,"sp"],
+    ["mm",1,1,1,512],
+    ["silu",1,1,1,0,512,512],
+    ["store",1,1,0,512,"sp"],
     ["mm",2,1,1,512],
     ["silu",2,1,1,0,512,512],
     ["store",2,1,0,512,"sp"],
-    ["mm",3,0,1,512],
-    ["silu",3,0,1,256,512,512],
-    ["store",3,0,0,512,"sp"],
-    ["mm",0,1,0,512],
-    ["silu",0,1,0,256,512,512],
-    ["store",0,1,0,512,"sp"],
-    ["mm",1,1,0,512],
-    ["silu",1,1,0,256,512,512],
-    ["store",1,1,0,512,"sp"],
-    ["mm",3,1,0,512],
-    ["silu",3,1,0,0,512,512],
+    ["mm",3,1,1,512],
+    ["silu",3,1,1,0,512,512],
     ["store",3,1,0,512,"sp"],
     ["cast",512,768,"v"],
-    ["quant",512,768],
     ["cast",768,1024,"v"],
+    ["quant",512,768],
     ["quant",768,1024],
-    ["mm",0,0,1,768],
-    ["silu",0,0,1,256,768,768],
-    ["mm",1,0,1,768],
-    ["silu",1,0,1,256,768,768],
-    ["mm",2,0,0,768],
-    ["silu",2,0,0,256,768,768],
-    ["mm",0,0,0,1024],
-    ["silu",0,0,0,768,1024,1024],
-    ["store",0,0,256,1024,"sp"],
-    ["mm",1,0,0,1024],
-    ["silu",1,0,0,768,1024,1024],
-    ["store",1,0,256,1024,"sp"],
-    ["mm",2,0,1,1024],
-    ["silu",2,0,1,768,1024,1024],
-    ["store",2,0,256,1024,"sp"],
-    ["mm",3,0,1,1024],
-    ["silu",3,0,1,512,1024,1024],
+    ["mm",0,0,0,768],
+    ["silu",0,0,0,256,768,768],
+    ["store",0,0,256,768,"sp"],
+    ["mm",1,0,0,768],
+    ["silu",1,0,0,256,768,768],
+    ["store",1,0,256,768,"sp"],
+    ["mm",2,0,0,1024],
+    ["silu",2,0,0,512,1024,1024],
+    ["store",2,0,512,1024,"sp"],
+    ["mm",3,0,0,1024],
+    ["silu",3,0,0,512,1024,1024],
     ["store",3,0,512,1024,"sp"],
     ["mm",0,1,1,1024],
     ["silu",0,1,1,512,1024,1024],
@@ -92,12 +81,18 @@ PROGRAM = [["load",0,"sp"],
     ["mm",1,1,1,1024],
     ["silu",1,1,1,512,1024,1024],
     ["store",1,1,512,1024,"sp"],
-    ["mm",2,1,0,1024],
-    ["silu",2,1,0,512,1024,1024],
+    ["mm",2,1,1,1024],
+    ["silu",2,1,1,512,1024,1024],
     ["store",2,1,512,1024,"sp"],
-    ["mm",3,1,0,1024],
-    ["silu",3,1,0,512,1024,1024],
-    ["store",3,1,512,1024,"sp"]]
+    ["mm",3,1,1,1024],
+    ["silu",3,1,1,512,1024,1024],
+    ["store",3,1,512,1024,"sp"],
+    ["mm",0,0,0,1024],
+    ["silu",0,0,0,768,1024,1024],
+    ["store",0,0,768,1024,"sp"],
+    ["mm",1,0,0,1024],
+    ["silu",1,0,0,768,1024,1024],
+    ["store",1,0,768,1024,"sp"]]
 
 
 def tile_rows_glin_silu_kernel(tc, x, w_words, w_scales, out):

@@ -19,9 +19,9 @@ ROWS = 32
 PACK = 4
 WINDOW = 512
 PAD = 256
-LOADS = [[0,256],[256,512],[512,1024]]
+LOADS = [[0,256],[256,512],[512,768],[768,1024]]
+STORES = [[0,1,1,0,256],[2,1,1,0,256],[4,1,1,0,256],[6,1,1,0,256],[1,2,2,0,256],[5,1,1,0,512],[7,1,1,0,512],[0,2,2,256,512],[4,2,2,256,512],[1,1,1,256,768],[3,1,1,256,768],[5,2,2,512,1024],[0,2,2,512,1024],[4,2,2,512,1024],[1,2,2,768,1024]]
 PROGRAM = [["load",0,"sp"],
-    ["warm"],
     ["words","sp"],
     ["wscale",0,"sp"],
     ["wscale",1,"sp"],
@@ -29,70 +29,81 @@ PROGRAM = [["load",0,"sp"],
     ["wscale",3,"sp"],
     ["load",1,"sp"],
     ["load",2,"sp"],
-    ["cast",0,168,"v"],
-    ["cast",168,256,"a"],
-    ["quant",0,256],
-    ["cast",256,424,"v"],
-    ["cast",424,512,"a"],
-    ["mm",0,0,0,256],
-    ["silu",0,0,0,0,256,256],
-    ["store",0,0,0,256,"sp"],
-    ["mm",1,0,0,256],
-    ["silu",1,0,0,0,256,256],
-    ["store",1,0,0,256,"sp"],
-    ["quant",256,512],
-    ["mm",2,0,0,512],
-    ["silu",2,0,0,0,512,512],
-    ["store",2,0,0,512,"sp"],
-    ["mm",3,0,0,512],
-    ["silu",3,0,0,0,512,512],
-    ["store",3,0,0,512,"sp"],
-    ["mm",0,1,1,512],
-    ["silu",0,1,1,0,512,512],
-    ["store",0,1,0,512,"sp"],
-    ["mm",1,1,1,512],
-    ["silu",1,1,1,0,512,512],
-    ["store",1,1,0,512,"sp"],
-    ["mm",2,1,1,512],
-    ["silu",2,1,1,0,512,512],
-    ["store",2,1,0,512,"sp"],
-    ["mm",3,1,1,512],
-    ["silu",3,1,1,0,512,512],
-    ["store",3,1,0,512,"sp"],
+    ["load",3,"sp"],
+    ["warm"],
+    ["cast",88,128,"a"],
+    ["cast",216,256,"a"],
+    ["cast",0,88,"v"],
+    ["cast",128,216,"v"],
+    ["quant",0,128],
+    ["quant",128,256],
+    ["cast",256,384,"v"],
+    ["cast",384,512,"v"],
+    ["quant",256,384],
+    ["quant",384,512],
     ["cast",512,768,"v"],
-    ["cast",768,1024,"v"],
     ["quant",512,768],
+    ["cast",768,1024,"v"],
     ["quant",768,1024],
-    ["mm",0,0,0,768],
-    ["silu",0,0,0,256,768,768],
-    ["store",0,0,256,768,"sp"],
-    ["mm",1,0,0,768],
-    ["silu",1,0,0,256,768,768],
-    ["store",1,0,256,768,"sp"],
-    ["mm",2,0,0,1024],
-    ["silu",2,0,0,512,1024,1024],
-    ["store",2,0,512,1024,"sp"],
-    ["mm",3,0,0,1024],
-    ["silu",3,0,0,512,1024,1024],
-    ["store",3,0,512,1024,"sp"],
-    ["mm",0,1,1,1024],
-    ["silu",0,1,1,512,1024,1024],
-    ["store",0,1,512,1024,"sp"],
-    ["mm",1,1,1,1024],
-    ["silu",1,1,1,512,1024,1024],
-    ["store",1,1,512,1024,"sp"],
+    ["mm",0,0,0,256],
+    ["silu",0,0,0,0,256],
+    ["store",0,"sp"],
+    ["mm",1,0,0,256],
+    ["silu",1,0,0,0,256],
+    ["store",1,"sp"],
+    ["mm",2,0,0,256],
+    ["silu",2,0,0,0,256],
+    ["store",2,"sp"],
+    ["mm",3,0,0,256],
+    ["silu",3,0,0,0,256],
+    ["store",3,"sp"],
+    ["mm",0,1,1,256],
+    ["silu",0,1,1,0,256],
+    ["mm",1,1,1,256],
+    ["silu",1,1,1,0,256],
+    ["store",4,"sp"],
+    ["mm",2,1,1,512],
+    ["silu",2,1,1,0,512],
+    ["store",5,"sp"],
+    ["mm",3,1,1,512],
+    ["silu",3,1,1,0,512],
+    ["store",6,"sp"],
+    ["mm",0,0,0,512],
+    ["silu",0,0,0,256,512],
+    ["mm",1,0,0,512],
+    ["silu",1,0,0,256,512],
+    ["store",7,"sp"],
+    ["mm",2,0,0,512],
+    ["silu",2,0,0,256,512],
+    ["mm",3,0,0,512],
+    ["silu",3,0,0,256,512],
+    ["store",8,"sp"],
+    ["mm",0,1,1,768],
+    ["silu",0,1,1,256,768],
+    ["store",9,"sp"],
+    ["mm",1,1,1,768],
+    ["silu",1,1,1,256,768],
+    ["store",10,"sp"],
     ["mm",2,1,1,1024],
-    ["silu",2,1,1,512,1024,1024],
-    ["store",2,1,512,1024,"sp"],
+    ["silu",2,1,1,512,1024],
     ["mm",3,1,1,1024],
-    ["silu",3,1,1,512,1024,1024],
-    ["store",3,1,512,1024,"sp"],
+    ["silu",3,1,1,512,1024],
+    ["store",11,"sp"],
     ["mm",0,0,0,1024],
-    ["silu",0,0,0,768,1024,1024],
-    ["store",0,0,768,1024,"sp"],
+    ["silu",0,0,0,512,1024],
     ["mm",1,0,0,1024],
-    ["silu",1,0,0,768,1024,1024],
-    ["store",1,0,768,1024,"sp"]]
+    ["silu",1,0,0,512,1024],
+    ["store",12,"sp"],
+    ["mm",2,0,0,1024],
+    ["silu",2,0,0,512,1024],
+    ["mm",3,0,0,1024],
+    ["silu",3,0,0,512,1024],
+    ["store",13,"sp"],
+    ["mm",0,1,1,1024],
+    ["silu",0,1,1,768,1024],
+    ["mm",1,1,1,1024],
+    ["silu",1,1,1,768,1024],
+    ["store",14,"sp"]]
 
 
 def tile_rows_glin_silu_kernel(tc, x, w_words, w_scales, out):
@@ -111,7 +122,8 @@ def tile_rows_glin_silu_kernel(tc, x, w_words, w_scales, out):
         wscales = keep.tile([P, M], U8, align_bytes=64)
         warm_in = keep.tile([P, 8], F32)
         warm_out = keep.tile([P, 8], F32)
-        result = {(g, t): keep.tile([P, N], F32, name="res%d%d" % (g, t), align_bytes=64) for g in range(G) for t in range(2)}
+        result = [keep.tile([P, n, c1 - c0], F32, name="res%d" % i, align_bytes=64) for i, (f, n, d, c0, c1) in enumerate(STORES)]
+        out_rows = out.rearrange("g (t s) n -> s (g t) n", s=P)
         banks = {(g, b): psum.tile([P, WINDOW], F32, name="bank%d%d" % (g, b)) for g in range(G) for b in range(2)}
         queues = {"sp": nc.sync, "act": nc.scalar, "pool": nc.gpsimd}
 
@@ -119,6 +131,12 @@ def tile_rows_glin_silu_kernel(tc, x, w_words, w_scales, out):
         nc.vector.memset(wscales[:].bitcast(I32), 0)
         nc.vector.memset(scales[:, 0:PAD].bitcast(I32), 0)
         nc.vector.memset(codes[:, 0:PAD], 0)
+
+        def target(slot, c0, c1):
+            for (f, n, d, s0, s1), t in zip(STORES, result):
+                if slot in range(f, f + n * d, d) and s0 <= c0 and c1 <= s1:
+                    return t[:, (slot - f) // d, c0 - s0 : c1 - s0]
+            raise ValueError("no such store")
 
         def source(c0, c1):
             for (l0, l1), t in zip(LOADS, raw):
@@ -167,12 +185,13 @@ def tile_rows_glin_silu_kernel(tc, x, w_words, w_scales, out):
                     stop=True,
                 )
             elif kind == "silu":
-                g, t, b, c0, c1, end = step[1:]
+                g, t, b, c0, c1 = step[1:]
+                end = c1
                 nc.scalar.activation(
-                    out=result[g, t][:, c0:c1],
+                    out=target(2 * g + t, c0, c1),
                     in_=banks[g, b][:, WINDOW - (end - c0) : WINDOW - (end - c1)],
                     func=ACT.Silu,
                 )
             else:
-                g, t, c0, c1 = step[1:5]
-                queues[step[5]].dma_start(out=out[g, P * t : P * (t + 1), c0:c1], in_=result[g, t][:, c0:c1])
+                f, n, d, c0, c1 = STORES[step[1]]
+                queues[step[2]].dma_start(out=out_rows[:, f : f + (n - 1) * d + 1 : d, c0:c1], in_=result[step[1]][:])

@@ -20,7 +20,7 @@ PACK = 4
 WINDOW = 512
 PAD = 256
 LOADS = [[0,256],[256,512],[512,768],[768,1024]]
-STORES = [[0,1,1,0,256],[2,1,1,0,256],[4,1,1,0,256],[6,1,1,0,256],[1,2,2,0,256],[5,1,1,0,512],[7,1,1,0,512],[0,2,2,256,512],[4,2,2,256,512],[1,1,1,256,768],[3,1,1,256,768],[5,2,2,512,1024],[0,2,2,512,1024],[4,2,2,512,1024],[1,2,2,768,1024]]
+STORES = [[0,2,2,0,256],[4,2,2,0,256],[1,2,2,0,256],[5,2,2,0,256],[0,2,2,256,512],[4,2,2,256,512],[1,2,2,256,768],[5,2,2,256,768],[0,2,2,512,1024],[4,2,2,512,1024],[1,4,2,768,1024]]
 PROGRAM = [["load",0,"sp"],
     ["words","sp"],
     ["wscale",0,"sp"],
@@ -47,63 +47,63 @@ PROGRAM = [["load",0,"sp"],
     ["quant",768,1024],
     ["mm",0,0,0,256],
     ["silu",0,0,0,0,256],
-    ["store",0,"sp"],
     ["mm",1,0,0,256],
     ["silu",1,0,0,0,256],
-    ["store",1,"sp"],
+    ["store",0,"sp"],
     ["mm",2,0,0,256],
     ["silu",2,0,0,0,256],
-    ["store",2,"sp"],
     ["mm",3,0,0,256],
     ["silu",3,0,0,0,256],
-    ["store",3,"sp"],
+    ["store",1,"sp"],
     ["mm",0,1,1,256],
     ["silu",0,1,1,0,256],
     ["mm",1,1,1,256],
     ["silu",1,1,1,0,256],
-    ["store",4,"sp"],
-    ["mm",2,1,1,512],
-    ["silu",2,1,1,0,512],
-    ["store",5,"sp"],
-    ["mm",3,1,1,512],
-    ["silu",3,1,1,0,512],
-    ["store",6,"sp"],
+    ["store",2,"sp"],
+    ["mm",2,1,1,256],
+    ["silu",2,1,1,0,256],
+    ["mm",3,1,1,256],
+    ["silu",3,1,1,0,256],
+    ["store",3,"sp"],
     ["mm",0,0,0,512],
     ["silu",0,0,0,256,512],
     ["mm",1,0,0,512],
     ["silu",1,0,0,256,512],
-    ["store",7,"sp"],
+    ["store",4,"sp"],
     ["mm",2,0,0,512],
     ["silu",2,0,0,256,512],
     ["mm",3,0,0,512],
     ["silu",3,0,0,256,512],
-    ["store",8,"sp"],
+    ["store",5,"sp"],
     ["mm",0,1,1,768],
     ["silu",0,1,1,256,768],
-    ["store",9,"sp"],
     ["mm",1,1,1,768],
     ["silu",1,1,1,256,768],
-    ["store",10,"sp"],
-    ["mm",2,1,1,1024],
-    ["silu",2,1,1,512,1024],
-    ["mm",3,1,1,1024],
-    ["silu",3,1,1,512,1024],
-    ["store",11,"sp"],
+    ["store",6,"sp"],
+    ["mm",2,1,1,768],
+    ["silu",2,1,1,256,768],
+    ["mm",3,1,1,768],
+    ["silu",3,1,1,256,768],
+    ["store",7,"sp"],
     ["mm",0,0,0,1024],
     ["silu",0,0,0,512,1024],
     ["mm",1,0,0,1024],
     ["silu",1,0,0,512,1024],
-    ["store",12,"sp"],
+    ["store",8,"sp"],
     ["mm",2,0,0,1024],
     ["silu",2,0,0,512,1024],
     ["mm",3,0,0,1024],
     ["silu",3,0,0,512,1024],
-    ["store",13,"sp"],
+    ["store",9,"sp"],
     ["mm",0,1,1,1024],
     ["silu",0,1,1,768,1024],
     ["mm",1,1,1,1024],
     ["silu",1,1,1,768,1024],
-    ["store",14,"sp"]]
+    ["mm",2,1,1,1024],
+    ["silu",2,1,1,768,1024],
+    ["mm",3,1,1,1024],
+    ["silu",3,1,1,768,1024],
+    ["store",10,"sp"]]
 
 
 def tile_rows_glin_silu_kernel(tc, x, w_words, w_scales, out):
@@ -114,15 +114,15 @@ def tile_rows_glin_silu_kernel(tc, x, w_words, w_scales, out):
         ctx.enter_context(tc.manual_schedule())
 
         x_rows = x.rearrange("g (p j) n -> (g p) j n", j=PACK)
-        raw = [keep.tile([P, PACK, c1 - c0], F32, name="raw%d" % c0, align_bytes=64) for c0, c1 in LOADS]
-        grouped = keep.tile([P, N, PACK], BF16, align_bytes=64)
-        codes = keep.tile([P, PAD + N], U32, align_bytes=64)
-        scales = keep.tile([P, PAD + N], U8, align_bytes=64)
-        words = keep.tile([P, 2 * M], U8, align_bytes=64)
-        wscales = keep.tile([P, M], U8, align_bytes=64)
+        raw = [keep.tile([P, PACK, c1 - c0], F32, name="raw%d" % c0, align_bytes=256) for c0, c1 in LOADS]
+        grouped = keep.tile([P, N, PACK], BF16, align_bytes=256)
+        codes = keep.tile([P, PAD + N], U32, align_bytes=256)
+        scales = keep.tile([P, PAD + N], U8, align_bytes=256)
+        words = keep.tile([P, 2 * M], U8, align_bytes=256)
+        wscales = keep.tile([P, M], U8, align_bytes=256)
         warm_in = keep.tile([P, 8], F32)
         warm_out = keep.tile([P, 8], F32)
-        result = [keep.tile([P, n, c1 - c0], F32, name="res%d" % i, align_bytes=64) for i, (f, n, d, c0, c1) in enumerate(STORES)]
+        result = [keep.tile([P, n, c1 - c0], F32, name="res%d" % i, align_bytes=256) for i, (f, n, d, c0, c1) in enumerate(STORES)]
         out_rows = out.rearrange("g (t s) n -> s (g t) n", s=P)
         banks = {(g, b): psum.tile([P, WINDOW], F32, name="bank%d%d" % (g, b)) for g in range(G) for b in range(2)}
         queues = {"sp": nc.sync, "act": nc.scalar, "pool": nc.gpsimd}

from contextlib import ExitStack

import concourse.mybir as mybir

G, D, M, N = 4, 128, 256, 1024
FLOPS = 2 * G * D * M * N

F32 = mybir.dt.float32
BF16 = mybir.dt.bfloat16
I32 = mybir.dt.int32
U32 = mybir.dt.uint32
U8 = mybir.dt.uint8
FP8X4 = mybir.dt.float8_e4m3fn_x4
FP4X4 = mybir.dt.float4_e2m1fn_x4
ACT = mybir.ActivationFunctionType

P = 128
ROWS = 32
PACK = 4
WINDOW = 512
PAD = 256
LOADS = [[0,256],[256,512],[512,768],[768,1024]]
STORES = [[0,2,2,0,256],[4,2,2,0,256],[1,2,2,0,256],[5,2,2,0,256],[0,2,2,256,512],[4,2,2,256,512],[1,2,2,256,768],[5,2,2,256,768],[0,2,2,512,1024],[4,2,2,512,1024],[1,4,2,768,1024]]
PROGRAM = [["load",0,"sp"],
    ["words","sp"],
    ["wscale",0,"sp"],
    ["wscale",1,"sp"],
    ["wscale",2,"sp"],
    ["wscale",3,"sp"],
    ["load",1,"sp"],
    ["load",2,"sp"],
    ["load",3,"sp"],
    ["warm"],
    ["cast",88,128,"a"],
    ["cast",216,256,"a"],
    ["cast",0,88,"v"],
    ["cast",128,216,"v"],
    ["quant",0,128],
    ["quant",128,256],
    ["cast",256,384,"v"],
    ["cast",384,512,"v"],
    ["quant",256,384],
    ["quant",384,512],
    ["cast",512,768,"v"],
    ["quant",512,768],
    ["cast",768,1024,"v"],
    ["quant",768,1024],
    ["mm",0,0,0,256],
    ["silu",0,0,0,0,256],
    ["mm",1,0,0,256],
    ["silu",1,0,0,0,256],
    ["store",0,"sp"],
    ["mm",2,0,0,256],
    ["silu",2,0,0,0,256],
    ["mm",3,0,0,256],
    ["silu",3,0,0,0,256],
    ["store",1,"sp"],
    ["mm",0,1,1,256],
    ["silu",0,1,1,0,256],
    ["mm",1,1,1,256],
    ["silu",1,1,1,0,256],
    ["store",2,"sp"],
    ["mm",2,1,1,256],
    ["silu",2,1,1,0,256],
    ["mm",3,1,1,256],
    ["silu",3,1,1,0,256],
    ["store",3,"sp"],
    ["mm",0,0,0,512],
    ["silu",0,0,0,256,512],
    ["mm",1,0,0,512],
    ["silu",1,0,0,256,512],
    ["store",4,"sp"],
    ["mm",2,0,0,512],
    ["silu",2,0,0,256,512],
    ["mm",3,0,0,512],
    ["silu",3,0,0,256,512],
    ["store",5,"sp"],
    ["mm",0,1,1,768],
    ["silu",0,1,1,256,768],
    ["mm",1,1,1,768],
    ["silu",1,1,1,256,768],
    ["store",6,"sp"],
    ["mm",2,1,1,768],
    ["silu",2,1,1,256,768],
    ["mm",3,1,1,768],
    ["silu",3,1,1,256,768],
    ["store",7,"sp"],
    ["mm",0,0,0,1024],
    ["silu",0,0,0,512,1024],
    ["mm",1,0,0,1024],
    ["silu",1,0,0,512,1024],
    ["store",8,"sp"],
    ["mm",2,0,0,1024],
    ["silu",2,0,0,512,1024],
    ["mm",3,0,0,1024],
    ["silu",3,0,0,512,1024],
    ["store",9,"sp"],
    ["mm",0,1,1,1024],
    ["silu",0,1,1,768,1024],
    ["mm",1,1,1,1024],
    ["silu",1,1,1,768,1024],
    ["mm",2,1,1,1024],
    ["silu",2,1,1,768,1024],
    ["mm",3,1,1,1024],
    ["silu",3,1,1,768,1024],
    ["store",10,"sp"]]


def tile_rows_glin_silu_kernel(tc, x, w_words, w_scales, out):
    nc = tc.nc
    with ExitStack() as ctx:
        keep = ctx.enter_context(tc.tile_pool(name="keep", bufs=1))
        psum = ctx.enter_context(tc.psum_pool(name="psum", bufs=1))
        ctx.enter_context(tc.manual_schedule())

        x_rows = x.rearrange("g (p j) n -> (g p) j n", j=PACK)
        raw = [keep.tile([P, PACK, c1 - c0], F32, name="raw%d" % c0, align_bytes=256) for c0, c1 in LOADS]
        grouped = keep.tile([P, N, PACK], BF16, align_bytes=256)
        codes = keep.tile([P, PAD + N], U32, align_bytes=256)
        scales = keep.tile([P, PAD + N], U8, align_bytes=256)
        words = keep.tile([P, 2 * M], U8, align_bytes=256)
        wscales = keep.tile([P, M], U8, align_bytes=256)
        warm_in = keep.tile([P, 8], F32)
        warm_out = keep.tile([P, 8], F32)
        result = [keep.tile([P, n, c1 - c0], F32, name="res%d" % i, align_bytes=256) for i, (f, n, d, c0, c1) in enumerate(STORES)]
        out_rows = out.rearrange("g (t s) n -> s (g t) n", s=P)
        banks = {(g, b): psum.tile([P, WINDOW], F32, name="bank%d%d" % (g, b)) for g in range(G) for b in range(2)}
        queues = {"sp": nc.sync, "act": nc.scalar, "pool": nc.gpsimd}

        nc.vector.memset(warm_in[:], 0.0)
        nc.vector.memset(wscales[:].bitcast(I32), 0)
        nc.vector.memset(scales[:, 0:PAD].bitcast(I32), 0)
        nc.vector.memset(codes[:, 0:PAD], 0)

        def target(slot, c0, c1):
            for (f, n, d, s0, s1), t in zip(STORES, result):
                if slot in range(f, f + n * d, d) and s0 <= c0 and c1 <= s1:
                    return t[:, (slot - f) // d, c0 - s0 : c1 - s0]
            raise ValueError("no such store")

        def source(c0, c1):
            for (l0, l1), t in zip(LOADS, raw):
                if l0 <= c0 and c1 <= l1:
                    return t[:, :, c0 - l0 : c1 - l0]
            raise ValueError("no such load")

        for step in PROGRAM:
            kind = step[0]
            if kind == "warm":
                nc.scalar.activation(out=warm_out[:, 0:1], in_=warm_in[:, 0:1], func=ACT.Silu)
            elif kind == "load":
                c0, c1 = LOADS[step[1]]
                queues[step[2]].dma_start(out=raw[step[1]][:], in_=x_rows[:, :, c0:c1])
            elif kind == "words":
                queues[step[1]].dma_start(out=words[:].bitcast(I32), in_=w_words.rearrange("g p b -> (g p) b").bitcast(I32))
            elif kind == "wscale":
                g = step[1]
                queues[step[2]].dma_start(out=wscales[ROWS * g : ROWS * g + 4, :].bitcast(I32), in_=w_scales[g].bitcast(I32))
            elif kind == "cast":
                c0, c1 = step[1], step[2]
                dst = grouped[:, c0:c1, :].rearrange("p (c i) t -> p c t i", i=4)
                src = source(c0, c1).rearrange("p t (c i) -> p c t i", i=4)
                if step[3] == "v":
                    nc.vector.tensor_copy(out=dst, in_=src)
                else:
                    nc.scalar.copy(out=dst, in_=src)
            elif kind == "quant":
                c0, c1 = step[1], step[2]
                nc.vector.quantize_mx(
                    out=codes[:, PAD + c0 : PAD + c1].bitcast(FP8X4),
                    scales=scales[:, PAD + c0 : PAD + c1],
                    in_=grouped[:, c0:c1, :].rearrange("p c t -> p (c t)"),
                )
            elif kind == "mm":
                g, t, b, c1 = step[1:]
                rows = slice(ROWS * g, ROWS * (g + 1))
                cols = slice(PAD + c1 - WINDOW, PAD + c1)
                nc.tensor.matmul_mx(
                    out=banks[g, b][:],
                    lhsT=words[rows, 2 * P * t : 2 * P * (t + 1)].bitcast(FP4X4),
                    lhsT_scale=wscales[rows, P * t : P * (t + 1)],
                    rhs=codes[rows, cols].bitcast(FP8X4),
                    rhs_scale=scales[rows, cols],
                    start=True,
                    stop=True,
                )
            elif kind == "silu":
                g, t, b, c0, c1 = step[1:]
                end = c1
                nc.scalar.activation(
                    out=target(2 * g + t, c0, c1),
                    in_=banks[g, b][:, WINDOW - (end - c0) : WINDOW - (end - c1)],
                    func=ACT.Silu,
                )
            else:
                f, n, d, c0, c1 = STORES[step[1]]
                queues[step[2]].dma_start(out=out_rows[:, f : f + (n - 1) * d + 1 : d, c0:c1], in_=result[step[1]][:])
